import numpy as np, ml_dtypes
CORES = [44,45,46,47,172,173,174,175,300,301,302,303,428,429,430,431]
N = 16
def setup_inputs(rng):
    m = (rng.standard_normal((N, 128, 128), dtype=np.float32) / 11).astype(ml_dtypes.bfloat16)
    return {"m": m, "mt": m.transpose(0, 2, 1).copy()}
def setup_inputs_low(rng):
    d = setup_inputs(rng)
    for k in ("m", "mt"): d[k] = (d[k].astype(np.float32) * 0.125).astype(d[k].dtype)
    return d
def reference(m, mt):
    M = m.astype(np.float64); p = M[0]
    for r in range(1, N):
        p = p @ M[r]
    p = p.astype(ml_dtypes.bfloat16)
    return {"y": np.broadcast_to(p, (N, 128, 128))}

@@ -1,0 +1,121 @@
+from concourse.bass import DstId, RemoteDMATransfer
+
+D = 128
+LEADERS = 2
+
+SCRATCH = {
+    "leaf": ("sbuf", [128, 8 * D], "bfloat16"),
+    "l1": ("sbuf", [128, 4 * D], "bfloat16"),
+    "l2": ("sbuf", [128, 2 * D], "bfloat16"),
+    "half": ("sbuf", [128, 2 * D], "bfloat16"),
+    "out": ("sbuf", [128, D], "bfloat16"),
+    "pA": ("psum", [128, 512], "float32"),
+    "pB": ("psum", [128, 512], "float32"),
+    "pC": ("psum", [128, 512], "float32"),
+    "pD": ("psum", [128, 512], "float32"),
+    "pE": ("psum", [128, 512], "float32"),
+    "pF": ("psum", [128, 512], "float32"),
+}
+SEMAPHORES = ["ld", "near", "far", "fin", "snt", "st",
+              "mA", "cA", "mB", "cB", "mC", "cC", "mD", "cD", "mE", "cE", "mF", "cF"]
+
+
+def _col(t, s, n=1):
+    return t[:, s * D:(s + n) * D]
+
+
+def _count(mask):
+    return bin(mask).count("1")
+
+
+def rank_program(g, core, T, topo):
+    if T.rank_of(core) is None:
+        return
+    S = T.sem
+
+    def place(c):
+        return (topo.host(c), topo.chip(c))
+
+    def rack(c):
+        return topo.rack(topo.host(c))
+
+    rackers = [c for c in T.cores if rack(c) == rack(core)]
+    chipers = [c for c in rackers if place(c) == place(core)]
+    others = [c for c in rackers if topo.same_plane(core, c)]
+    cabled = [c for c in T.cores if rack(c) != rack(core) and topo.may_write(core, c)]
+    slot = rackers.index(core)
+    side = 0 if rackers[0] == T.cores[0] else 1
+    local = chipers.index(core)
+    span = len(chipers) // LEADERS
+    leader = local % span == 0
+
+    def xfer(dsts, mask, sem, ap):
+        ids = []
+        for d in dsts:
+            rid, pid = topo.addr(d, core)
+            ids.append(DstId(rid=rid, pnc=pid))
+        return RemoteDMATransfer(dst_ids=ids, dma_engine_mask=mask, remote_sem=sem,
+                                 srcs=[ap], dsts=[ap for _ in dsts], alu_op=0)
+
+    off = topo.mask(core, others[0])
+    on = topo.mask(core, [c for c in chipers if c != core][0]) & ~off
+    sent = 0
+
+    mine = _col(T.leaf, slot)
+    g.sync.dma_start(mine, (T.mt if slot % 2 == 0 else T.m)[:, :]).then_inc(S.ld, 16)
+    near = [c for c in chipers[::span] if c != core]
+    calls = [xfer(others[::span], off, S.far, mine)]
+    sent += _count(off)
+    if near:
+        calls.append(xfer(near, on, S.near, mine))
+        sent += _count(on)
+    g.wait_ge(S.ld, 16)
+    g.remote_dma_fused(calls, local_sem=S.snt)
+
+    def node(out, left_t, right_n, transposed, sem):
+        if transposed:
+            g.tensor.matmul(out, right_n, left_t, True, True).then_inc(sem, 1)
+        else:
+            g.tensor.matmul(out, left_t, right_n, True, True).then_inc(sem, 1)
+
+    if leader:
+        def quad(q, p1, m1, c1, p2, m2, c2):
+            for j in (2 * q, 2 * q + 1):
+                node(_col(p1, j % 2), _col(T.leaf, 2 * j), _col(T.leaf, 2 * j + 1), j % 2 == 0, m1)
+            g.vector.wait_ge(m1, 2)
+            g.vector.tensor_copy(_col(T.l1, 2 * q, 2), _col(p1, 0, 2)).then_inc(c1, 1)
+            g.tensor.wait_ge(c1, 1)
+            node(_col(p2, 0), _col(T.l1, 2 * q), _col(T.l1, 2 * q + 1), q % 2 == 0, m2)
+            g.vector.wait_ge(m2, 1)
+            g.vector.tensor_copy(_col(T.l2, q), _col(p2, 0)).then_inc(c2, 1)
+
+        q_own = slot // len(chipers)
+        g.tensor.wait_ge(S.ld, 16)
+        g.tensor.wait_ge(S.near, (len(chipers) - 1) * _count(on))
+        quad(q_own, T.pA, S.mA, S.cA, T.pB, S.mB, S.cB)
+        g.tensor.wait_ge(S.far, len(others) * _count(off))
+        quad(1 - q_own, T.pC, S.mC, S.cC, T.pD, S.mD, S.cD)
+        g.tensor.wait_ge(S.cB, 1)
+        g.tensor.wait_ge(S.cD, 1)
+        node(_col(T.pE, 0), _col(T.l2, 0), _col(T.l2, 1), side == 0, S.mE)
+        g.vector.wait_ge(S.mE, 1)
+        g.vector.tensor_copy(_col(T.half, side), _col(T.pE, 0)).then_inc(S.cE, 1)
+
+        off2 = topo.mask(core, cabled[0])
+        calls = [xfer(cabled[local:local + span], off2, S.fin, _col(T.half, side))]
+        sent += _count(off2)
+        if span > 1:
+            calls.append(xfer(chipers[local + 1:local + span], on, S.fin, _col(T.half, side)))
+            sent += _count(on)
+        g.wait_ge(S.cE, 1)
+        g.remote_dma_fused(calls, local_sem=S.snt)
+        g.tensor.wait_ge(S.cE, 1)
+
+    g.tensor.wait_ge(S.fin, _count(topo.mask(cabled[0], core)) + (0 if leader else _count(on)))
+    node(_col(T.pF, 0), _col(T.half, 0), _col(T.half, 1), False, S.mF)
+    g.vector.wait_ge(S.mF, 1)
+    g.vector.tensor_copy(T.out[:, :], _col(T.pF, 0)).then_inc(S.cF, 1)
+    g.sync.wait_ge(S.cF, 1)
+    g.sync.dma_start(T.y[:, :], T.out[:, :]).then_inc(S.st, 16)
+    g.sync.wait_ge(S.st, 16)
+    g.wait_ge(S.snt, sent)

@@ -5,8 +5,12 @@ LEADERS = 2
 
 SCRATCH = {
     "leaf": ("sbuf", [128, 8 * D], "bfloat16"),
+    "cleaf": ("sbuf", [128, 4 * D], "bfloat16"),
     "l1": ("sbuf", [128, 4 * D], "bfloat16"),
     "l2": ("sbuf", [128, 2 * D], "bfloat16"),
+    "c1": ("sbuf", [128, 2 * D], "bfloat16"),
+    "c2": ("sbuf", [128, D], "bfloat16"),
+    "piece": ("sbuf", [128, D], "bfloat16"),
     "half": ("sbuf", [128, 2 * D], "bfloat16"),
     "out": ("sbuf", [128, D], "bfloat16"),
     "pA": ("psum", [128, 512], "float32"),
@@ -15,9 +19,12 @@ SCRATCH = {
     "pD": ("psum", [128, 512], "float32"),
     "pE": ("psum", [128, 512], "float32"),
     "pF": ("psum", [128, 512], "float32"),
+    "pG": ("psum", [128, 512], "float32"),
+    "pH": ("psum", [128, 512], "float32"),
 }
-SEMAPHORES = ["ld", "near", "far", "fin", "snt", "st",
-              "mA", "cA", "mB", "cB", "mC", "cC", "mD", "cD", "mE", "cE", "mF", "cF"]
+SEMAPHORES = ["ld", "near", "far", "cab", "fin", "snt", "st",
+              "mA", "cA", "mB", "cB", "mC", "cC", "mD", "cD", "mE", "cE", "mF", "cF",
+              "mG", "cG", "mH", "cH", "mP", "cP"]
 
 
 def _col(t, s, n=1):
@@ -26,6 +33,11 @@ def _col(t, s, n=1):
 
 def _count(mask):
     return bin(mask).count("1")
+
+
+def _take(mask, n):
+    bits = [1 << b for b in range(mask.bit_length()) if mask >> b & 1]
+    return sum(bits[:n])
 
 
 def rank_program(g, core, T, topo):
@@ -48,27 +60,32 @@ def rank_program(g, core, T, topo):
     local = chipers.index(core)
     span = len(chipers) // LEADERS
     leader = local % span == 0
+    chief = local == 0
+    mine_r = [T.rank_of(c) for c in chipers]
+    cab_r = [T.rank_of(c) for c in cabled]
+    inner = min(cab_r) == max(mine_r) + 1 or max(cab_r) + 1 == min(mine_r)
 
-    def xfer(dsts, mask, sem, ap):
+    def xfer(dsts, mask, sem, src, dst):
         ids = []
         for d in dsts:
             rid, pid = topo.addr(d, core)
             ids.append(DstId(rid=rid, pnc=pid))
         return RemoteDMATransfer(dst_ids=ids, dma_engine_mask=mask, remote_sem=sem,
-                                 srcs=[ap], dsts=[ap for _ in dsts], alu_op=0)
+                                 srcs=[src], dsts=[dst for _ in dsts], alu_op=0)
 
-    off = topo.mask(core, others[0])
-    on = topo.mask(core, [c for c in chipers if c != core][0]) & ~off
+    leave = topo.mask(core, others[0]) & topo.mask(core, cabled[0])
+    on = topo.mask(core, [c for c in chipers if c != core][0]) & ~leave
+    sw = _take(leave, _count(leave) // 2)
+    cb = leave & ~sw
     sent = 0
 
     mine = _col(T.leaf, slot)
     g.sync.dma_start(mine, (T.mt if slot % 2 == 0 else T.m)[:, :]).then_inc(S.ld, 16)
     near = [c for c in chipers[::span] if c != core]
-    calls = [xfer(others[::span], off, S.far, mine)]
-    sent += _count(off)
-    if near:
-        calls.append(xfer(near, on, S.near, mine))
-        sent += _count(on)
+    calls = [xfer([cabled[0]], cb, S.cab, mine, _col(T.cleaf, local)),
+             xfer(others[::span], sw, S.far, mine, mine),
+             xfer(near, on, S.near, mine, mine)]
+    sent += _count(cb) + _count(sw) + _count(on)
     g.wait_ge(S.ld, 16)
     g.remote_dma_fused(calls, local_sem=S.snt)
 
@@ -78,40 +95,58 @@ def rank_program(g, core, T, topo):
         else:
             g.tensor.matmul(out, left_t, right_n, True, True).then_inc(sem, 1)
 
-    if leader:
-        def quad(q, p1, m1, c1, p2, m2, c2):
-            for j in (2 * q, 2 * q + 1):
-                node(_col(p1, j % 2), _col(T.leaf, 2 * j), _col(T.leaf, 2 * j + 1), j % 2 == 0, m1)
-            g.vector.wait_ge(m1, 2)
-            g.vector.tensor_copy(_col(T.l1, 2 * q, 2), _col(p1, 0, 2)).then_inc(c1, 1)
-            g.tensor.wait_ge(c1, 1)
-            node(_col(p2, 0), _col(T.l1, 2 * q), _col(T.l1, 2 * q + 1), q % 2 == 0, m2)
-            g.vector.wait_ge(m2, 1)
-            g.vector.tensor_copy(_col(T.l2, q), _col(p2, 0)).then_inc(c2, 1)
+    def quad(leaves, first, transposed, p1, m1, c1, mid, at, p2, m2, c2, res):
+        for j in (0, 1):
+            node(_col(p1, j), _col(leaves, first + 2 * j), _col(leaves, first + 2 * j + 1), j == 0, m1)
+        g.vector.wait_ge(m1, 2)
+        g.vector.tensor_copy(_col(mid, at, 2), _col(p1, 0, 2)).then_inc(c1, 1)
+        g.tensor.wait_ge(c1, 1)
+        node(_col(p2, 0), _col(mid, at), _col(mid, at + 1), transposed, m2)
+        g.vector.wait_ge(m2, 1)
+        g.vector.tensor_copy(res, _col(p2, 0)).then_inc(c2, 1)
 
-        q_own = slot // len(chipers)
+    if leader:
+        n = len(chipers)
+        q_own = slot // n
+        q_far = 1 - q_own
         g.tensor.wait_ge(S.ld, 16)
-        g.tensor.wait_ge(S.near, (len(chipers) - 1) * _count(on))
-        quad(q_own, T.pA, S.mA, S.cA, T.pB, S.mB, S.cB)
-        g.tensor.wait_ge(S.far, len(others) * _count(off))
-        quad(1 - q_own, T.pC, S.mC, S.cC, T.pD, S.mD, S.cD)
+        g.tensor.wait_ge(S.near, (n - 1) * _count(on))
+        quad(T.leaf, n * q_own, q_own == 0, T.pA, S.mA, S.cA, T.l1, 2 * q_own, T.pB, S.mB, S.cB, _col(T.l2, q_own))
+        g.tensor.wait_ge(S.far, n * _count(sw))
+        quad(T.leaf, n * q_far, q_far == 0, T.pC, S.mC, S.cC, T.l1, 2 * q_far, T.pD, S.mD, S.cD, _col(T.l2, q_far))
         g.tensor.wait_ge(S.cB, 1)
         g.tensor.wait_ge(S.cD, 1)
         node(_col(T.pE, 0), _col(T.l2, 0), _col(T.l2, 1), side == 0, S.mE)
         g.vector.wait_ge(S.mE, 1)
         g.vector.tensor_copy(_col(T.half, side), _col(T.pE, 0)).then_inc(S.cE, 1)
 
-        off2 = topo.mask(core, cabled[0])
-        calls = [xfer(cabled[local:local + span], off2, S.fin, _col(T.half, side))]
-        sent += _count(off2)
-        if span > 1:
-            calls.append(xfer(chipers[local + 1:local + span], on, S.fin, _col(T.half, side)))
-            sent += _count(on)
         g.wait_ge(S.cE, 1)
-        g.remote_dma_fused(calls, local_sem=S.snt)
+        g.remote_dma_fused([xfer([cabled[local]], cb, S.fin, _col(T.half, side), _col(T.half, side))], local_sem=S.snt)
+        sent += _count(cb)
         g.tensor.wait_ge(S.cE, 1)
 
-    g.tensor.wait_ge(S.fin, _count(topo.mask(cabled[0], core)) + (0 if leader else _count(on)))
+    if chief:
+        g.tensor.wait_ge(S.cab, len(cabled) * _count(cb))
+        quad(T.cleaf, 0, side == 1, T.pG, S.mG, S.cG, T.c1, 0, T.pH, S.mH, S.cH, T.c2[:, :])
+        if inner:
+            g.tensor.wait_ge(S.cH, 1)
+            if side == 0:
+                node(_col(T.pA, 0), _col(T.half, 0), T.c2[:, :], True, S.mP)
+            else:
+                node(_col(T.pA, 0), T.c2[:, :], _col(T.half, 1), False, S.mP)
+            g.vector.wait_ge(S.mP, 1)
+            g.vector.tensor_copy(T.piece[:, :], _col(T.pA, 0)).then_inc(S.cP, 1)
+            g.wait_ge(S.cP, 1)
+            src, where = T.piece[:, :], side
+        else:
+            g.wait_ge(S.cH, 1)
+            src, where = T.c2[:, :], 1 - side
+        g.remote_dma_fused([xfer([c for c in others if c not in others[::span]], leave, S.fin, src, _col(T.half, where)),
+                            xfer([c for c in chipers if c not in chipers[::span]], on, S.fin, src, _col(T.half, where))],
+                           local_sem=S.snt)
+        sent += _count(leave) + _count(on)
+
+    g.tensor.wait_ge(S.fin, _count(cb) if leader else _count(leave) + _count(on))
     node(_col(T.pF, 0), _col(T.half, 0), _col(T.half, 1), False, S.mF)
     g.vector.wait_ge(S.mF, 1)
     g.vector.tensor_copy(T.out[:, :], _col(T.pF, 0)).then_inc(S.cF, 1)

@@ -1,34 +1,29 @@
 from concourse.bass import DstId, RemoteDMATransfer
 
 D = 128
-LEADERS = 2
+H = D // 2
 
 SCRATCH = {
-    "leaf": ("sbuf", [128, 8 * D], "bfloat16"),
-    "cleaf": ("sbuf", [128, 4 * D], "bfloat16"),
-    "l1": ("sbuf", [128, 4 * D], "bfloat16"),
-    "l2": ("sbuf", [128, 2 * D], "bfloat16"),
-    "c1": ("sbuf", [128, 2 * D], "bfloat16"),
-    "c2": ("sbuf", [128, D], "bfloat16"),
-    "piece": ("sbuf", [128, D], "bfloat16"),
+    "leaf": ("sbuf", [128, 4 * D], "bfloat16"),
+    "l1": ("sbuf", [128, 2 * D], "bfloat16"),
+    "own": ("sbuf", [128, D], "bfloat16"),
+    "opp": ("sbuf", [128, D], "bfloat16"),
+    "oth": ("sbuf", [128, D], "bfloat16"),
+    "cab": ("sbuf", [128, D], "bfloat16"),
+    "hf": ("sbuf", [128, D], "bfloat16"),
     "half": ("sbuf", [128, 2 * D], "bfloat16"),
     "out": ("sbuf", [128, D], "bfloat16"),
-    "pA": ("psum", [128, 512], "float32"),
-    "pB": ("psum", [128, 512], "float32"),
-    "pC": ("psum", [128, 512], "float32"),
-    "pD": ("psum", [128, 512], "float32"),
-    "pE": ("psum", [128, 512], "float32"),
-    "pF": ("psum", [128, 512], "float32"),
-    "pG": ("psum", [128, 512], "float32"),
-    "pH": ("psum", [128, 512], "float32"),
+    "p0": ("psum", [128, 512], "float32"),
+    "p1": ("psum", [128, 512], "float32"),
+    "p2": ("psum", [128, 512], "float32"),
+    "p3": ("psum", [128, 512], "float32"),
+    "p4": ("psum", [128, 512], "float32"),
+    "p5": ("psum", [128, 512], "float32"),
+    "p6": ("psum", [128, 512], "float32"),
+    "p7": ("psum", [128, 512], "float32"),
 }
-SEMAPHORES = ["ld", "near", "far", "cab", "fin", "snt", "st",
-              "mA", "cA", "mB", "cB", "mC", "cC", "mD", "cD", "mE", "cE", "mF", "cF",
-              "mG", "cG", "mH", "cH", "mP", "cP"]
-
-
-def _col(t, s, n=1):
-    return t[:, s * D:(s + n) * D]
+SEMAPHORES = ["ld", "near", "sw2", "cb2", "fin", "snt", "st"] + \
+             [p + k + str(h) for k in "xyoshtf" for p in "mc" for h in (0, 1)]
 
 
 def _count(mask):
@@ -38,6 +33,18 @@ def _count(mask):
 def _take(mask, n):
     bits = [1 << b for b in range(mask.bit_length()) if mask >> b & 1]
     return sum(bits[:n])
+
+
+def _full(o):
+    return o[0][:, o[1] * D:(o[1] + 1) * D]
+
+
+def _part(o, h):
+    return o[0][:, o[1] * D + h * H:o[1] * D + (h + 1) * H]
+
+
+def _waits(o):
+    return o[2][0] + o[2][1]
 
 
 def rank_program(g, core, T, topo):
@@ -55,15 +62,15 @@ def rank_program(g, core, T, topo):
     chipers = [c for c in rackers if place(c) == place(core)]
     others = [c for c in rackers if topo.same_plane(core, c)]
     cabled = [c for c in T.cores if rack(c) != rack(core) and topo.may_write(core, c)]
-    slot = rackers.index(core)
+    n = len(chipers)
     side = 0 if rackers[0] == T.cores[0] else 1
+    q = rackers.index(core) // n
     local = chipers.index(core)
-    span = len(chipers) // LEADERS
-    leader = local % span == 0
-    chief = local == 0
     mine_r = [T.rank_of(c) for c in chipers]
     cab_r = [T.rank_of(c) for c in cabled]
     inner = min(cab_r) == max(mine_r) + 1 or max(cab_r) + 1 == min(mine_r)
+    switch_first = local % 2 == 0
+    peer_sw, peer_cb = others[local], cabled[local]
 
     def xfer(dsts, mask, sem, src, dst):
         ids = []
@@ -73,84 +80,93 @@ def rank_program(g, core, T, topo):
         return RemoteDMATransfer(dst_ids=ids, dma_engine_mask=mask, remote_sem=sem,
                                  srcs=[src], dsts=[dst for _ in dsts], alu_op=0)
 
-    leave = topo.mask(core, others[0]) & topo.mask(core, cabled[0])
-    on = topo.mask(core, [c for c in chipers if c != core][0]) & ~leave
+    sent = [0]
+
+    def send(transfers, masks):
+        g.remote_dma_fused(transfers, local_sem=S.snt)
+        sent[0] += sum(_count(k) for k in masks)
+
+    def landed(t, slot, sem, val):
+        return (t, slot, ([(sem, val)], [(sem, val)]))
+
+    def prod(key, banks, t, slot, left_t, right_n, transposed):
+        lhs, rhs = (right_n, left_t) if transposed else (left_t, right_n)
+        res = (t, slot, ([(S["c" + key + "0"], 1)], [(S["c" + key + "1"], 1)]))
+        for s, v in _waits(lhs):
+            g.tensor.wait_ge(s, v)
+        for h in (0, 1):
+            for s, v in rhs[2][h]:
+                g.tensor.wait_ge(s, v)
+            m = S["m" + key + str(h)]
+            g.tensor.matmul(banks[h][:, 0:H], _full(lhs), _part(rhs, h), True, True).then_inc(m, 1)
+            g.vector.wait_ge(m, 1)
+            g.vector.tensor_copy(_part(res, h), banks[h][:, 0:H]).then_inc(S["c" + key + str(h)], 1)
+        return res
+
+    def ready(o):
+        for s, v in _waits(o):
+            g.wait_ge(s, v)
+
+    near = [c for c in chipers if c != core]
+    chipm = topo.mask(core, near[0])
+    leave = topo.mask(core, peer_sw) & topo.mask(core, peer_cb)
     sw = _take(leave, _count(leave) // 2)
     cb = leave & ~sw
-    sent = 0
 
-    mine = _col(T.leaf, slot)
-    g.sync.dma_start(mine, (T.mt if slot % 2 == 0 else T.m)[:, :]).then_inc(S.ld, 16)
-    near = [c for c in chipers[::span] if c != core]
-    calls = [xfer([cabled[0]], cb, S.cab, mine, _col(T.cleaf, local)),
-             xfer(others[::span], sw, S.far, mine, mine),
-             xfer(near, on, S.near, mine, mine)]
-    sent += _count(cb) + _count(sw) + _count(on)
+    mine = T.leaf[:, local * D:(local + 1) * D]
+    g.sync.dma_start(mine, (T.mt if local % 2 == 0 else T.m)[:, :]).then_inc(S.ld, 16)
     g.wait_ge(S.ld, 16)
-    g.remote_dma_fused(calls, local_sem=S.snt)
+    send([xfer(near, chipm, S.near, mine, mine)], [chipm])
 
-    def node(out, left_t, right_n, transposed, sem):
-        if transposed:
-            g.tensor.matmul(out, right_n, left_t, True, True).then_inc(sem, 1)
+    here = [(S.ld, 16), (S.near, (n - 1) * _count(chipm))]
+    leaf = [(T.leaf, j, (here, here)) for j in range(n)]
+    both = inner and not switch_first
+    first_tr = (q != 0) if both else (q == 0)
+    two = {}
+    for j in ((1, 0) if first_tr else (0, 1)):
+        two[j] = prod("xy"[j], [T.p0, T.p1] if j == 0 else [T.p2, T.p3], T.l1, j, leaf[2 * j], leaf[2 * j + 1], j == 0)
+    if both:
+        opp = prod("o", [T.p6, T.p7], T.opp, 0, two[0], two[1], q != 0)
+    own = prod("s", [T.p4, T.p5], T.own, 0, two[0], two[1], q == 0)
+
+    piece = {}
+    if switch_first:
+        ready(own)
+        send([xfer([peer_sw], leave, S.sw2, _full(own), T.oth[:, :])], [leave])
+        oth = landed(T.oth, 0, S.sw2, _count(leave))
+        pair = (own, oth) if q == 0 else (oth, own)
+        piece[side] = prod("h", [T.p0, T.p1], T.half, side, pair[0], pair[1], side == 0)
+        ready(piece[side])
+        send([xfer([peer_cb], leave, S.fin, _full(piece[side]), _full(piece[side]))], [leave])
+        piece[1 - side] = landed(T.half, 1 - side, S.fin, _count(leave))
+    elif inner:
+        ready(opp)
+        send([xfer([peer_cb], leave, S.cb2, _full(opp), T.cab[:, :])], [leave])
+        oth = landed(T.oth, 0, S.sw2, _count(sw))
+        cab = landed(T.cab, 0, S.cb2, _count(leave))
+        pair = (own, oth) if q == 0 else (oth, own)
+        hf = prod("h", [T.p0, T.p1], T.hf, 0, pair[0], pair[1], side == 0)
+        if side == 0:
+            piece[side] = prod("t", [T.p2, T.p3], T.half, side, hf, cab, True)
         else:
-            g.tensor.matmul(out, left_t, right_n, True, True).then_inc(sem, 1)
+            piece[side] = prod("t", [T.p2, T.p3], T.half, side, cab, hf, False)
+        ready(piece[side])
+        send([xfer([peer_sw], leave, S.fin, _full(piece[side]), _full(piece[side]))], [leave])
+        piece[1 - side] = landed(T.half, 1 - side, S.fin, _count(leave))
+    else:
+        piece[side] = landed(T.half, side, S.fin, _count(leave))
+        piece[1 - side] = landed(T.half, 1 - side, S.cb2, _count(cb))
+        ready(own)
+        send([xfer([peer_cb], cb, S.cb2, _full(own), _full(piece[side])),
+              xfer([peer_sw], sw, S.sw2, _full(own), T.oth[:, :])], [cb, sw])
+        ready(piece[1 - side])
+        send([xfer([peer_sw], leave, S.fin, _full(piece[1 - side]), _full(piece[1 - side]))], [leave])
 
-    def quad(leaves, first, transposed, p1, m1, c1, mid, at, p2, m2, c2, res):
-        for j in (0, 1):
-            node(_col(p1, j), _col(leaves, first + 2 * j), _col(leaves, first + 2 * j + 1), j == 0, m1)
-        g.vector.wait_ge(m1, 2)
-        g.vector.tensor_copy(_col(mid, at, 2), _col(p1, 0, 2)).then_inc(c1, 1)
-        g.tensor.wait_ge(c1, 1)
-        node(_col(p2, 0), _col(mid, at), _col(mid, at + 1), transposed, m2)
-        g.vector.wait_ge(m2, 1)
-        g.vector.tensor_copy(res, _col(p2, 0)).then_inc(c2, 1)
-
-    if leader:
-        n = len(chipers)
-        q_own = slot // n
-        q_far = 1 - q_own
-        g.tensor.wait_ge(S.ld, 16)
-        g.tensor.wait_ge(S.near, (n - 1) * _count(on))
-        quad(T.leaf, n * q_own, q_own == 0, T.pA, S.mA, S.cA, T.l1, 2 * q_own, T.pB, S.mB, S.cB, _col(T.l2, q_own))
-        g.tensor.wait_ge(S.far, n * _count(sw))
-        quad(T.leaf, n * q_far, q_far == 0, T.pC, S.mC, S.cC, T.l1, 2 * q_far, T.pD, S.mD, S.cD, _col(T.l2, q_far))
-        g.tensor.wait_ge(S.cB, 1)
-        g.tensor.wait_ge(S.cD, 1)
-        node(_col(T.pE, 0), _col(T.l2, 0), _col(T.l2, 1), side == 0, S.mE)
-        g.vector.wait_ge(S.mE, 1)
-        g.vector.tensor_copy(_col(T.half, side), _col(T.pE, 0)).then_inc(S.cE, 1)
-
-        g.wait_ge(S.cE, 1)
-        g.remote_dma_fused([xfer([cabled[local]], cb, S.fin, _col(T.half, side), _col(T.half, side))], local_sem=S.snt)
-        sent += _count(cb)
-        g.tensor.wait_ge(S.cE, 1)
-
-    if chief:
-        g.tensor.wait_ge(S.cab, len(cabled) * _count(cb))
-        quad(T.cleaf, 0, side == 1, T.pG, S.mG, S.cG, T.c1, 0, T.pH, S.mH, S.cH, T.c2[:, :])
-        if inner:
-            g.tensor.wait_ge(S.cH, 1)
-            if side == 0:
-                node(_col(T.pA, 0), _col(T.half, 0), T.c2[:, :], True, S.mP)
-            else:
-                node(_col(T.pA, 0), T.c2[:, :], _col(T.half, 1), False, S.mP)
-            g.vector.wait_ge(S.mP, 1)
-            g.vector.tensor_copy(T.piece[:, :], _col(T.pA, 0)).then_inc(S.cP, 1)
-            g.wait_ge(S.cP, 1)
-            src, where = T.piece[:, :], side
-        else:
-            g.wait_ge(S.cH, 1)
-            src, where = T.c2[:, :], 1 - side
-        g.remote_dma_fused([xfer([c for c in others if c not in others[::span]], leave, S.fin, src, _col(T.half, where)),
-                            xfer([c for c in chipers if c not in chipers[::span]], on, S.fin, src, _col(T.half, where))],
-                           local_sem=S.snt)
-        sent += _count(leave) + _count(on)
-
-    g.tensor.wait_ge(S.fin, _count(cb) if leader else _count(leave) + _count(on))
-    node(_col(T.pF, 0), _col(T.half, 0), _col(T.half, 1), False, S.mF)
-    g.vector.wait_ge(S.mF, 1)
-    g.vector.tensor_copy(T.out[:, :], _col(T.pF, 0)).then_inc(S.cF, 1)
-    g.sync.wait_ge(S.cF, 1)
+    for s, v in _waits(own):
+        g.tensor.wait_ge(s, v)
+    y = prod("f", [T.p4, T.p5], T.out, 0, piece[0], piece[1], False)
+    for s, v in _waits(y):
+        g.sync.wait_ge(s, v)
     g.sync.dma_start(T.y[:, :], T.out[:, :]).then_inc(S.st, 16)
     g.sync.wait_ge(S.st, 16)
-    g.wait_ge(S.snt, sent)
+    g.wait_ge(S.snt, sent[0])

from concourse.bass import DstId, RemoteDMATransfer

D = 128
H = D // 2

SCRATCH = {
    "leaf": ("sbuf", [128, 4 * D], "bfloat16"),
    "l1": ("sbuf", [128, 2 * D], "bfloat16"),
    "own": ("sbuf", [128, D], "bfloat16"),
    "opp": ("sbuf", [128, D], "bfloat16"),
    "oth": ("sbuf", [128, D], "bfloat16"),
    "cab": ("sbuf", [128, D], "bfloat16"),
    "hf": ("sbuf", [128, D], "bfloat16"),
    "half": ("sbuf", [128, 2 * D], "bfloat16"),
    "out": ("sbuf", [128, D], "bfloat16"),
    "p0": ("psum", [128, 512], "float32"),
    "p1": ("psum", [128, 512], "float32"),
    "p2": ("psum", [128, 512], "float32"),
    "p3": ("psum", [128, 512], "float32"),
    "p4": ("psum", [128, 512], "float32"),
    "p5": ("psum", [128, 512], "float32"),
    "p6": ("psum", [128, 512], "float32"),
    "p7": ("psum", [128, 512], "float32"),
}
SEMAPHORES = ["ld", "near", "sw2", "cb2", "fin", "snt", "st"] + \
             [p + k + str(h) for k in "xyoshtf" for p in "mc" for h in (0, 1)]


def _count(mask):
    return bin(mask).count("1")


def _take(mask, n):
    bits = [1 << b for b in range(mask.bit_length()) if mask >> b & 1]
    return sum(bits[:n])


def _full(o):
    return o[0][:, o[1] * D:(o[1] + 1) * D]


def _part(o, h):
    return o[0][:, o[1] * D + h * H:o[1] * D + (h + 1) * H]


def _waits(o):
    return o[2][0] + o[2][1]


def rank_program(g, core, T, topo):
    if T.rank_of(core) is None:
        return
    S = T.sem

    def place(c):
        return (topo.host(c), topo.chip(c))

    def rack(c):
        return topo.rack(topo.host(c))

    rackers = [c for c in T.cores if rack(c) == rack(core)]
    chipers = [c for c in rackers if place(c) == place(core)]
    others = [c for c in rackers if topo.same_plane(core, c)]
    cabled = [c for c in T.cores if rack(c) != rack(core) and topo.may_write(core, c)]
    n = len(chipers)
    side = 0 if rackers[0] == T.cores[0] else 1
    q = rackers.index(core) // n
    local = chipers.index(core)
    mine_r = [T.rank_of(c) for c in chipers]
    cab_r = [T.rank_of(c) for c in cabled]
    inner = min(cab_r) == max(mine_r) + 1 or max(cab_r) + 1 == min(mine_r)
    switch_first = local % 2 == 0
    peer_sw, peer_cb = others[local], cabled[local]

    def xfer(dsts, mask, sem, src, dst):
        ids = []
        for d in dsts:
            rid, pid = topo.addr(d, core)
            ids.append(DstId(rid=rid, pnc=pid))
        return RemoteDMATransfer(dst_ids=ids, dma_engine_mask=mask, remote_sem=sem,
                                 srcs=[src], dsts=[dst for _ in dsts], alu_op=0)

    sent = [0]

    def send(transfers, masks):
        g.remote_dma_fused(transfers, local_sem=S.snt)
        sent[0] += sum(_count(k) for k in masks)

    def landed(t, slot, sem, val):
        return (t, slot, ([(sem, val)], [(sem, val)]))

    def prod(key, banks, t, slot, left_t, right_n, transposed):
        lhs, rhs = (right_n, left_t) if transposed else (left_t, right_n)
        res = (t, slot, ([(S["c" + key + "0"], 1)], [(S["c" + key + "1"], 1)]))
        for s, v in _waits(lhs):
            g.tensor.wait_ge(s, v)
        for h in (0, 1):
            for s, v in rhs[2][h]:
                g.tensor.wait_ge(s, v)
            m = S["m" + key + str(h)]
            g.tensor.matmul(banks[h][:, 0:H], _full(lhs), _part(rhs, h), True, True).then_inc(m, 1)
            g.vector.wait_ge(m, 1)
            g.vector.tensor_copy(_part(res, h), banks[h][:, 0:H]).then_inc(S["c" + key + str(h)], 1)
        return res

    def ready(o):
        for s, v in _waits(o):
            g.wait_ge(s, v)

    near = [c for c in chipers if c != core]
    chipm = topo.mask(core, near[0])
    leave = topo.mask(core, peer_sw) & topo.mask(core, peer_cb)
    sw = _take(leave, _count(leave) // 2)
    cb = leave & ~sw

    mine = T.leaf[:, local * D:(local + 1) * D]
    g.sync.dma_start(mine, (T.mt if local % 2 == 0 else T.m)[:, :]).then_inc(S.ld, 16)
    g.wait_ge(S.ld, 16)
    send([xfer(near, chipm, S.near, mine, mine)], [chipm])

    here = [(S.ld, 16), (S.near, (n - 1) * _count(chipm))]
    leaf = [(T.leaf, j, (here, here)) for j in range(n)]
    both = inner and not switch_first
    first_tr = (q != 0) if both else (q == 0)
    two = {}
    for j in ((1, 0) if first_tr else (0, 1)):
        two[j] = prod("xy"[j], [T.p0, T.p1] if j == 0 else [T.p2, T.p3], T.l1, j, leaf[2 * j], leaf[2 * j + 1], j == 0)
    if both:
        opp = prod("o", [T.p6, T.p7], T.opp, 0, two[0], two[1], q != 0)
    own = prod("s", [T.p4, T.p5], T.own, 0, two[0], two[1], q == 0)

    piece = {}
    if switch_first:
        ready(own)
        send([xfer([peer_sw], leave, S.sw2, _full(own), T.oth[:, :])], [leave])
        oth = landed(T.oth, 0, S.sw2, _count(leave))
        pair = (own, oth) if q == 0 else (oth, own)
        piece[side] = prod("h", [T.p0, T.p1], T.half, side, pair[0], pair[1], side == 0)
        ready(piece[side])
        send([xfer([peer_cb], leave, S.fin, _full(piece[side]), _full(piece[side]))], [leave])
        piece[1 - side] = landed(T.half, 1 - side, S.fin, _count(leave))
    elif inner:
        ready(opp)
        send([xfer([peer_cb], leave, S.cb2, _full(opp), T.cab[:, :])], [leave])
        oth = landed(T.oth, 0, S.sw2, _count(sw))
        cab = landed(T.cab, 0, S.cb2, _count(leave))
        pair = (own, oth) if q == 0 else (oth, own)
        hf = prod("h", [T.p0, T.p1], T.hf, 0, pair[0], pair[1], side == 0)
        if side == 0:
            piece[side] = prod("t", [T.p2, T.p3], T.half, side, hf, cab, True)
        else:
            piece[side] = prod("t", [T.p2, T.p3], T.half, side, cab, hf, False)
        ready(piece[side])
        send([xfer([peer_sw], leave, S.fin, _full(piece[side]), _full(piece[side]))], [leave])
        piece[1 - side] = landed(T.half, 1 - side, S.fin, _count(leave))
    else:
        piece[side] = landed(T.half, side, S.fin, _count(leave))
        piece[1 - side] = landed(T.half, 1 - side, S.cb2, _count(cb))
        ready(own)
        send([xfer([peer_cb], cb, S.cb2, _full(own), _full(piece[side])),
              xfer([peer_sw], sw, S.sw2, _full(own), T.oth[:, :])], [cb, sw])
        ready(piece[1 - side])
        send([xfer([peer_sw], leave, S.fin, _full(piece[1 - side]), _full(piece[1 - side]))], [leave])

    for s, v in _waits(own):
        g.tensor.wait_ge(s, v)
    y = prod("f", [T.p4, T.p5], T.out, 0, piece[0], piece[1], False)
    for s, v in _waits(y):
        g.sync.wait_ge(s, v)
    g.sync.dma_start(T.y[:, :], T.out[:, :]).then_inc(S.st, 16)
    g.sync.wait_ge(S.st, 16)
    g.wait_ge(S.snt, sent[0])
